import numpy as np
import ml_dtypes


def mxq(x, axis, fmt="e4m3"):
    dtype, down = {"e4m3": (ml_dtypes.float8_e4m3fn, 7), "e5m2": (ml_dtypes.float8_e5m2, 14)}[fmt]
    v = np.moveaxis(np.asarray(x, np.float32).astype(ml_dtypes.bfloat16).astype(np.float64), axis, -1)
    blocks = v.reshape(v.shape[:-1] + (-1, 32))
    amax = np.abs(blocks).max(-1, keepdims=True)
    byte = np.maximum(np.where(amax > 0, np.frexp(amax)[1] - 1 + 127, 0) - down, 1)
    scale = np.exp2(byte - 127.0)
    codes = (blocks / scale).astype(np.float32).astype(dtype).astype(np.float64)
    return np.moveaxis((codes * scale).reshape(v.shape), -1, axis)


WIDE = False


def mx_kscale(k):
    if not WIDE:
        return np.ones(k)
    levels = np.array([30, -30])
    if k % 512:
        return np.exp2(np.random.permutation(np.resize(levels, k // 32))).repeat(32)
    a = np.empty((k // 512, 16))
    for p in range(k // 512):
        a[p, :8] = np.random.permutation(np.resize(levels, 8))
        for g in range(8):
            far = levels[np.abs(levels - a[p, g]) >= 10]
            a[p, g + 8] = far[np.random.randint(len(far))]
    return np.exp2(a.ravel()).repeat(32)


def f64(x):
    return np.asarray(x).astype(np.float64)


def striped(idx):
    return np.tile(np.asarray(idx).reshape(-1, 16).T, (8, 1)).astype(np.uint16)


def unstriped(offs):
    return offs[:16].T.reshape(-1).astype(np.int64)


E2M1 = np.array([0.0, 0.5, 1.0, 1.5, 2.0, 3.0, 4.0, 6.0, -0.0, -0.5, -1.0, -1.5, -2.0, -3.0, -4.0, -6.0])


def pack_weight(w, fmt):
    k, n = w.shape
    w = f64(np.asarray(w, np.float32).astype(ml_dtypes.bfloat16)).reshape(k // 32, 32, n)
    amax = np.abs(w).max(1)
    if fmt in ("e4m3", "e5m2"):
        byte = np.frexp(amax)[1] - 1 + 127 - (7 if fmt == "e4m3" else 14)
    else:
        mant, ex = np.frexp(amax / 6.0)
        byte = np.where(mant > 0.5, ex, ex - 1) + 127
    byte = np.clip(np.where(amax > 0, byte, 1), 1, 254)
    scaled = (w * np.exp2(127.0 - byte)[:, None, :]).reshape(k, n).astype(np.float32)
    by_word = np.ascontiguousarray(scaled.reshape(k // 512, 128, 4, n).transpose(0, 1, 3, 2))
    if fmt in ("e4m3", "e5m2"):
        words = by_word.astype(ml_dtypes.float8_e4m3fn if fmt == "e4m3" else ml_dtypes.float8_e5m2).view(np.uint8)
    else:
        c = by_word.astype(ml_dtypes.float4_e2m1fn).view(np.uint8) & 0xF
        words = (c[..., 0::2] | (c[..., 1::2] << 4)).reshape(k // 512, 128, 2 * n)
    return np.ascontiguousarray(words), np.ascontiguousarray(byte.astype(np.uint8).reshape(k // 512, 16, n))


def unpack_weight(words, scales, fmt):
    g, _, n = scales.shape
    words = np.ascontiguousarray(words).reshape(g, 128, n, -1)
    if fmt in ("e4m3", "e5m2"):
        vals = words.view(ml_dtypes.float8_e4m3fn if fmt == "e4m3" else ml_dtypes.float8_e5m2).astype(np.float64)
    else:
        nib = np.empty((g, 128, n, 4), np.uint8)
        nib[..., 0::2] = words & 0xF
        nib[..., 1::2] = words >> 4
        vals = E2M1[nib]
    vals = vals * np.repeat(np.exp2(scales.astype(np.float64) - 127.0), 8, axis=1)[..., None]
    return vals.transpose(0, 1, 3, 2).reshape(g * 512, n)


def sigmoid(v):
    return 1.0 / (1.0 + np.exp(-v))


def sgn(shape):
    return np.random.uniform(0.5, 2.0, shape) * np.where(np.random.standard_normal(shape) < 0, -1.0, 1.0)


K, T, J, R, F, Z, X, O, N, U = 512, 1024, 256, 512, 512, 1024, 1024, 256, 256, 128


def setup_inputs():
    n = np.random.standard_normal
    idx = np.random.permutation(T)[:J]
    idx2 = np.random.permutation(Z)[:J]
    idx3 = np.random.permutation(X)[:O]
    idx4 = np.random.permutation(X)[:O]
    idx5 = np.random.permutation(J)[:O]
    idx6 = np.random.permutation(O)[:U]
    idx7 = np.random.permutation(O)[:U]
    fk = mx_kscale(K)
    ff = mx_kscale(F)
    fr = mx_kscale(R)
    xtp = pack_weight(n((K, T)) / fk[:, None], "e5m2")
    xop = pack_weight(n((F, Z)) / ff[:, None], "e4m3")
    wp = pack_weight(n((K, R)) * 1 / np.sqrt(K) * fk[:, None], "e2m1")
    w0p = pack_weight(n((F, R)) * 1 / np.sqrt(F) * ff[:, None], "e2m1")
    wbp = pack_weight(n((R, N)) * 1 / np.sqrt(R) / fr[:, None], "e2m1")
    return {
        "xt_words": xtp[0],
        "xt_scales": xtp[1],
        "xo_words": xop[0],
        "xo_scales": xop[1],
        "w_words": wp[0],
        "w_scales": wp[1],
        "w0_words": w0p[0],
        "w0_scales": w0p[1],
        "tb": (np.random.randint(-7, 8, (R, X)).astype(np.float64)).astype(np.float32),
        "st": (np.random.uniform(0.15, 0.35, (R, 1)) * fr[:, None]).astype(np.float32),
        "sa": (np.random.uniform(0.5, 1.6, (R, 1)) * fr[:, None]).astype(np.float32),
        "sg": (0.3 * sgn((R, 1))).astype(np.float32),
        "bg": (np.random.uniform(-2.0, 2.0, (R, 1))).astype(np.float32),
        "wb_words": wbp[0],
        "wb_scales": wbp[1],
        "so": (np.random.uniform(0.5, 1.6, (N, 1))).astype(np.float32),
        "sp": (sgn((N, 1))).astype(np.float32),
        "bo": (np.random.uniform(-2.0, 2.0, (N, 1))).astype(np.float32),
        "offs": striped(idx),
        "offs2": striped(idx2),
        "offs3": striped(idx3),
        "offs4": striped(idx4),
        "offs5": striped(idx5),
        "offs6": striped(idx6),
        "offs7": striped(idx7),
    }


def reference(xt_words, xt_scales, xo_words, xo_scales, w_words, w_scales, w0_words, w0_scales, tb, st, sa, sg, bg, wb_words, wb_scales, so, sp, bo, offs, offs2, offs3, offs4, offs5, offs6, offs7):
    idx = unstriped(offs)
    idx2 = unstriped(offs2)
    idx3 = unstriped(offs3)
    idx4 = unstriped(offs4)
    idx5 = unstriped(offs5)
    idx6 = unstriped(offs6)
    idx7 = unstriped(offs7)
    xtu = unpack_weight(xt_words, xt_scales, "e5m2")
    xou = unpack_weight(xo_words, xo_scales, "e4m3")
    wu = unpack_weight(w_words, w_scales, "e2m1")
    w0u = unpack_weight(w0_words, w0_scales, "e2m1")
    wbu = unpack_weight(wb_words, wb_scales, "e2m1")
    xtidxg = xtu[:, idx]
    xoidx2g = xou[:, idx2]
    a = wu.T @ xtidxg + w0u.T @ xoidx2g
    u1 = f64(tb)[:, idx3] * f64(st) * sigmoid(f64(tb)[:, idx4] * f64(sg) + f64(bg))
    hid = np.maximum(u1, a[:, idx5] * f64(sa))
    hidq = mxq(hid, 0, "e4m3")
    p = wbu.T @ hidq
    y = p[:, idx6] * f64(so) * sigmoid(p[:, idx7] * f64(sp) + f64(bo))
    return y

@@ -1,0 +1,216 @@
+from contextlib import ExitStack
+
+import concourse.mybir as mybir
+
+F32 = mybir.dt.float32
+BF16 = mybir.dt.bfloat16
+I32 = mybir.dt.int32
+U32 = mybir.dt.uint32
+U16 = mybir.dt.uint16
+U8 = mybir.dt.uint8
+E4M3X4 = mybir.dt.float8_e4m3fn_x4
+E5M2X4 = mybir.dt.float8_e5m2_x4
+E2M1X4 = mybir.dt.float4_e2m1fn_x4
+ACT = mybir.ActivationFunctionType
+ALU = mybir.AluOpType
+
+P = 128
+PACK = 4
+QUADS = 4
+T, J, R, X, O, N, U = 1024, 256, 512, 1024, 256, 256, 128
+HALF = O // 2
+FLOPS = 2 * (2 * 512 * R * J + R * N * O)
+
+
+def tile_list_gatedlevels_bank_one_gatedout_kernel(
+    tc, xt_words, xt_scales, xo_words, xo_scales, w_words, w_scales, w0_words, w0_scales,
+    tb, st, sa, sg, bg, wb_words, wb_scales, so, sp, bo,
+    offs, offs2, offs3, offs4, offs5, offs6, offs7, out,
+):
+    nc = tc.nc
+    with ExitStack() as ctx:
+        sb = ctx.enter_context(tc.tile_pool(name="sb", bufs=1))
+        ps = ctx.enter_context(tc.psum_pool(name="ps", bufs=1))
+
+        def tile(name, shape, dtype):
+            return sb.tile(shape, dtype, name=name, align_bytes=64)
+
+        def load_list(name, src):
+            t = sb.tile(list(src.shape), U16, name=name)
+            nc.sync.dma_start(t[:], src)
+            return t
+
+        def load_words(name, src, dtype, columns):
+            t = tile(name, [P, columns], dtype)
+            nc.sync.dma_start(t[:].bitcast(I32), src.bitcast(I32))
+            return t
+
+        def by_quadrant(scales):
+            return scales[0].bitcast(I32).rearrange("(q r) n -> r q n", r=4)
+
+        def load_r_vector(name, src, queue):
+            t = tile(name, [P, PACK], F32)
+            queue.dma_start(t[:], src.rearrange("(p t) o -> p (t o)", t=PACK))
+            return t
+
+        def load_n_vector(name, src):
+            t = tile(name, [P, 2], F32)
+            with nc.allow_non_contiguous_dma(reason="one value a partition"):
+                nc.sync.dma_start(t[:], src.rearrange("(h p) o -> p (h o)", p=P))
+            return t
+
+        tb_rows = tb.rearrange("(p t) x -> t p x", t=PACK)
+
+        def load_tb(t):
+            rows = tile("tb%d" % t, [P, X], F32)
+            nc.sync.dma_start(rows[:], tb_rows[t])
+            return rows
+
+        w_stage = tile("w_stage", [P, QUADS, 2, R // 4], I32)
+        xt_plane = tile("xt_plane", [P, T], U8)
+        xo_plane = tile("xo_plane", [P, T], U8)
+        wb_plane = tile("wb_plane", [P, N], U8)
+        nc.vector.memset(w_stage[64:96], 0)
+        nc.vector.memset(xt_plane[:].bitcast(I32), 0)
+        nc.vector.memset(xo_plane[:].bitcast(I32), 0)
+        nc.vector.memset(wb_plane[:].bitcast(I32), 0)
+
+        xt_stage = tile("xt_stage", [4, QUADS, T // 4], I32)
+        xo_stage = tile("xo_stage", [4, QUADS, T // 4], I32)
+        nc.sync.dma_start(xt_stage[:], by_quadrant(xt_scales))
+        nc.sync.dma_start(xo_stage[:], by_quadrant(xo_scales))
+        sg_t = load_r_vector("sg_t", sg, nc.gpsimd)
+        bg_t = load_r_vector("bg_t", bg, nc.gpsimd)
+        st_t = load_r_vector("st_t", st, nc.gpsimd)
+        tb_t = [load_tb(0)]
+        nc.scalar.dma_start(w_stage[64:68, :, 0, :], by_quadrant(w_scales))
+        nc.scalar.dma_start(w_stage[64:68, :, 1, :], by_quadrant(w0_scales))
+        l4 = load_list("l4", offs4)
+        l3 = load_list("l3", offs3)
+        xt_w = load_words("xt_w", xt_words[0].rearrange("p n t -> p (n t)"), U32, T)
+        l1 = load_list("l1", offs)
+        l2 = load_list("l2", offs2)
+        xo_w = load_words("xo_w", xo_words[0].rearrange("p n t -> p (n t)"), U32, T)
+        w_w = load_words("w_w", w_words[0], U8, 2 * R)
+        w0_w = load_words("w0_w", w0_words[0], U8, 2 * R)
+        for t in range(1, PACK):
+            tb_t.append(load_tb(t))
+        l5 = load_list("l5", offs5)
+        sa_t = load_r_vector("sa_t", sa, nc.sync)
+        wb_w = load_words("wb_w", wb_words[0], U8, 2 * N)
+        for q in range(QUADS):
+            nc.sync.dma_start(
+                wb_plane[32 * q : 32 * q + 4, :].bitcast(I32),
+                wb_scales[0, 4 * q : 4 * q + 4, :].bitcast(I32),
+            )
+        l7 = load_list("l7", offs7)
+        l6 = load_list("l6", offs6)
+        sp_t = load_n_vector("sp_t", sp)
+        bo_t = load_n_vector("bo_t", bo)
+        so_t = load_n_vector("so_t", so)
+
+        for stage, plane in ((xt_stage, xt_plane), (xo_stage, xo_plane)):
+            for q in range(QUADS):
+                nc.vector.tensor_copy(plane[32 * q : 32 * q + 4, :].bitcast(I32), stage[:, q, :])
+        w_plane = tile("w_plane", [P, 2 * R], U8)
+        for q in range(QUADS):
+            nc.vector.tensor_copy(
+                w_plane[32 * q : 32 * q + 32, :].bitcast(I32),
+                w_stage[64:96, q].rearrange("p m n -> p (m n)"),
+            )
+        w_sc = tile("w_sc", [P, 2, PACK, P], U8)
+        nc.vector.tensor_copy(w_sc[:], w_plane[:].rearrange("p (m c t) -> p m t c", m=2, t=PACK))
+
+        gate = [tile("gate%d" % t, [P, O], F32) for t in range(PACK)]
+        level = [tile("level%d" % t, [P, O], F32) for t in range(PACK)]
+        u1 = tile("u1", [P, PACK, O], F32)
+
+        def look_up_levels(t):
+            nc.scalar.activation(
+                gate[t][:], tb_t[t][:].indirect(l4[:]), ACT.Sigmoid,
+                bias=bg_t[:, t : t + 1], scale=sg_t[:, t : t + 1],
+            )
+            nc.scalar.activation(level[t][:], tb_t[t][:].indirect(l3[:]), ACT.Copy, scale=st_t[:, t : t + 1])
+
+        look_up_levels(0)
+        w_d = []
+        for name, src in (("w_d", w_w), ("w0_d", w0_w)):
+            dealt = tile(name, [P, 2 * R], U8)
+            nc.scalar.copy(
+                dealt[:].bitcast(U16).rearrange("p (t c) -> p t c", t=PACK),
+                src[:].bitcast(U16).rearrange("p (c t) -> p t c", t=PACK),
+            )
+            w_d.append(dealt)
+        for t in range(1, PACK):
+            look_up_levels(t)
+
+        picked = []
+        for name, words, plane, lst in (("xt", xt_w, xt_plane, l1), ("xo", xo_w, xo_plane, l2)):
+            g_sc = tile(name + "_gs", [P, J], U8)
+            g_w = tile(name + "_gw", [P, J], U32)
+            nc.vector.tensor_copy(g_sc[:], plane[:].indirect(lst[:]))
+            nc.vector.tensor_copy(g_w[:], words[:].indirect(lst[:]))
+            picked.append((g_w, g_sc))
+        a_ps = [ps.tile([P, J], F32, name="a_ps%d" % t) for t in range(PACK)]
+        for m, fmt in enumerate((E5M2X4, E4M3X4)):
+            g_w, g_sc = picked[m]
+            for t in range(PACK):
+                nc.tensor.matmul_mx(
+                    a_ps[t][:],
+                    lhsT=w_d[m][:, 2 * P * t : 2 * P * (t + 1)].bitcast(E2M1X4),
+                    lhsT_scale=w_sc[:, m, t, :],
+                    rhs=g_w[:].bitcast(fmt),
+                    rhs_scale=g_sc[:],
+                    start=(m == 0),
+                    stop=(m == 1),
+                )
+        nc.vector.tensor_tensor(u1[:, 0, :], level[0][:], gate[0][:], ALU.mult)
+        a_sb = [tile("a_sb%d" % t, [P, J], F32) for t in range(PACK)]
+        for t in range(PACK):
+            nc.vector.tensor_copy(a_sb[t][:], a_ps[t][:])
+        for t in range(1, PACK):
+            nc.vector.tensor_tensor(u1[:, t, :], level[t][:], gate[t][:], ALU.mult)
+
+        p_sb = [tile("p_sb%d" % h, [P, O], F32) for h in range(2)]
+        for half in range(2):
+            cols = slice(half * HALF, (half + 1) * HALF)
+            a_pick = tile("a_pick%d" % half, [P, PACK, HALF], F32)
+            for t in range(PACK):
+                nc.scalar.activation(
+                    a_pick[:, t, :], a_sb[t][:].indirect(l5[:, 8 * half : 8 * half + 8]), ACT.Copy,
+                    scale=sa_t[:, t : t + 1],
+                )
+            hid = tile("hid%d" % half, [P, HALF * PACK], BF16)
+            nc.vector.tensor_tensor(
+                hid[:].rearrange("p (c i t) -> p c t i", i=4, t=PACK),
+                u1[:, :, cols].rearrange("p t (c i) -> p c t i", i=4),
+                a_pick[:].rearrange("p t (c i) -> p c t i", i=4),
+                ALU.max,
+            )
+            codes = tile("codes%d" % half, [P, HALF], U32)
+            scales = tile("scales%d" % half, [P, HALF], U8)
+            nc.vector.quantize_mx(codes[:].bitcast(E4M3X4), scales[:], hid[:])
+            for h in range(2):
+                p_ps = ps.tile([P, HALF], F32, name="p_ps%d%d" % (half, h))
+                nc.tensor.matmul_mx(
+                    p_ps[:],
+                    lhsT=wb_w[:, 2 * P * h : 2 * P * (h + 1)].bitcast(E2M1X4),
+                    lhsT_scale=wb_plane[:, P * h : P * (h + 1)],
+                    rhs=codes[:].bitcast(E4M3X4),
+                    rhs_scale=scales[:],
+                    start=True,
+                    stop=True,
+                )
+                nc.vector.tensor_copy(p_sb[h][:, cols], p_ps[:])
+
+        for h in range(2):
+            g = tile("out_gate%d" % h, [P, U], F32)
+            v = tile("out_value%d" % h, [P, U], F32)
+            y = tile("y%d" % h, [P, U], F32)
+            nc.scalar.activation(
+                g[:], p_sb[h][:].indirect(l7[:]), ACT.Sigmoid,
+                bias=bo_t[:, h : h + 1], scale=sp_t[:, h : h + 1],
+            )
+            nc.scalar.activation(v[:], p_sb[h][:].indirect(l6[:]), ACT.Copy, scale=so_t[:, h : h + 1])
+            nc.vector.tensor_tensor(y[:], v[:], g[:], ALU.mult)
+            nc.sync.dma_start(out[P * h : P * (h + 1), :], y[:])

@@ -32,8 +32,8 @@ def tile_list_gatedlevels_bank_one_gatedout_kernel(
         sb = ctx.enter_context(tc.tile_pool(name="sb", bufs=1))
         ps = ctx.enter_context(tc.psum_pool(name="ps", bufs=1))
 
-        def tile(name, shape, dtype):
-            return sb.tile(shape, dtype, name=name, align_bytes=64)
+        def tile(name, shape, dtype, tag=None):
+            return sb.tile(shape, dtype, name=name, tag=tag or name, align_bytes=64)
 
         def load_list(name, src):
             t = sb.tile(list(src.shape), U16, name=name)
@@ -79,22 +79,23 @@ def tile_list_gatedlevels_bank_one_gatedout_kernel(
         xo_stage = tile("xo_stage", [4, QUADS, T // 4], I32)
         nc.sync.dma_start(xt_stage[:], by_quadrant(xt_scales))
         nc.sync.dma_start(xo_stage[:], by_quadrant(xo_scales))
-        sg_t = load_r_vector("sg_t", sg, nc.gpsimd)
         bg_t = load_r_vector("bg_t", bg, nc.gpsimd)
         st_t = load_r_vector("st_t", st, nc.gpsimd)
-        tb_t = [load_tb(0)]
-        nc.scalar.dma_start(w_stage[64:68, :, 0, :], by_quadrant(w_scales))
-        nc.scalar.dma_start(w_stage[64:68, :, 1, :], by_quadrant(w0_scales))
         l4 = load_list("l4", offs4)
-        l3 = load_list("l3", offs3)
-        xt_w = load_words("xt_w", xt_words[0].rearrange("p n t -> p (n t)"), U32, T)
-        l1 = load_list("l1", offs)
-        l2 = load_list("l2", offs2)
-        xo_w = load_words("xo_w", xo_words[0].rearrange("p n t -> p (n t)"), U32, T)
+        sg_t = load_r_vector("sg_t", sg, nc.sync)
+        tb_t = [load_tb(0)]
+        nc.sync.dma_start(w_stage[64:68, :, 0, :], by_quadrant(w_scales))
+        nc.sync.dma_start(w_stage[64:68, :, 1, :], by_quadrant(w0_scales))
+        tb_t.append(load_tb(1))
         w_w = load_words("w_w", w_words[0], U8, 2 * R)
         w0_w = load_words("w0_w", w0_words[0], U8, 2 * R)
-        for t in range(1, PACK):
-            tb_t.append(load_tb(t))
+        l1 = load_list("l1", offs)
+        l2 = load_list("l2", offs2)
+        xt_w = load_words("xt_w", xt_words[0].rearrange("p n t -> p (n t)"), U32, T)
+        l3 = load_list("l3", offs3)
+        xo_w = load_words("xo_w", xo_words[0].rearrange("p n t -> p (n t)"), U32, T)
+        tb_t.append(load_tb(2))
+        tb_t.append(load_tb(3))
         l5 = load_list("l5", offs5)
         sa_t = load_r_vector("sa_t", sa, nc.sync)
         wb_w = load_words("wb_w", wb_words[0], U8, 2 * N)
@@ -109,8 +110,8 @@ def tile_list_gatedlevels_bank_one_gatedout_kernel(
         bo_t = load_n_vector("bo_t", bo)
         so_t = load_n_vector("so_t", so)
 
-        for stage, plane in ((xt_stage, xt_plane), (xo_stage, xo_plane)):
-            for q in range(QUADS):
+        for q in range(QUADS):
+            for stage, plane in ((xo_stage, xo_plane), (xt_stage, xt_plane)):
                 nc.vector.tensor_copy(plane[32 * q : 32 * q + 4, :].bitcast(I32), stage[:, q, :])
         w_plane = tile("w_plane", [P, 2 * R], U8)
         for q in range(QUADS):
@@ -121,36 +122,37 @@ def tile_list_gatedlevels_bank_one_gatedout_kernel(
         w_sc = tile("w_sc", [P, 2, PACK, P], U8)
         nc.vector.tensor_copy(w_sc[:], w_plane[:].rearrange("p (m c t) -> p m t c", m=2, t=PACK))
 
-        gate = [tile("gate%d" % t, [P, O], F32) for t in range(PACK)]
-        level = [tile("level%d" % t, [P, O], F32) for t in range(PACK)]
-        u1 = tile("u1", [P, PACK, O], F32)
+        gate = tile("gate", [P, PACK, O], F32)
+        level = tile("level", [P, PACK, O], F32)
 
         def look_up_levels(t):
             nc.scalar.activation(
-                gate[t][:], tb_t[t][:].indirect(l4[:]), ACT.Sigmoid,
+                gate[:, t, :], tb_t[t][:].indirect(l4[:]), ACT.Sigmoid,
                 bias=bg_t[:, t : t + 1], scale=sg_t[:, t : t + 1],
             )
-            nc.scalar.activation(level[t][:], tb_t[t][:].indirect(l3[:]), ACT.Copy, scale=st_t[:, t : t + 1])
+            nc.scalar.activation(level[:, t, :], tb_t[t][:].indirect(l3[:]), ACT.Copy, scale=st_t[:, t : t + 1])
 
-        look_up_levels(0)
-        w_d = []
-        for name, src in (("w_d", w_w), ("w0_d", w0_w)):
+        def pick(name, words, plane, lst):
+            g_sc = tile(name + "_gs", [P, J], U8)
+            g_w = tile(name + "_gw", [P, J], U32)
+            nc.vector.tensor_copy(g_sc[:], plane[:].indirect(lst[:]))
+            nc.vector.tensor_copy(g_w[:], words[:].indirect(lst[:]))
+            return g_w, g_sc
+
+        def deal(name, src):
             dealt = tile(name, [P, 2 * R], U8)
             nc.scalar.copy(
                 dealt[:].bitcast(U16).rearrange("p (t c) -> p t c", t=PACK),
                 src[:].bitcast(U16).rearrange("p (c t) -> p t c", t=PACK),
             )
-            w_d.append(dealt)
-        for t in range(1, PACK):
-            look_up_levels(t)
+            return dealt
 
-        picked = []
-        for name, words, plane, lst in (("xt", xt_w, xt_plane, l1), ("xo", xo_w, xo_plane, l2)):
-            g_sc = tile(name + "_gs", [P, J], U8)
-            g_w = tile(name + "_gw", [P, J], U32)
-            nc.vector.tensor_copy(g_sc[:], plane[:].indirect(lst[:]))
-            nc.vector.tensor_copy(g_w[:], words[:].indirect(lst[:]))
-            picked.append((g_w, g_sc))
+        look_up_levels(0)
+        look_up_levels(1)
+        w_d = [deal("w_d", w_w), deal("w0_d", w0_w)]
+        look_up_levels(2)
+        look_up_levels(3)
+        picked = [pick("xt", xt_w, xt_plane, l1), pick("xo", xo_w, xo_plane, l2)]
         a_ps = [ps.tile([P, J], F32, name="a_ps%d" % t) for t in range(PACK)]
         for m, fmt in enumerate((E5M2X4, E4M3X4)):
             g_w, g_sc = picked[m]
@@ -164,12 +166,15 @@ def tile_list_gatedlevels_bank_one_gatedout_kernel(
                     start=(m == 0),
                     stop=(m == 1),
                 )
-        nc.vector.tensor_tensor(u1[:, 0, :], level[0][:], gate[0][:], ALU.mult)
+        u1_first = tile("u1_first", [P, O], F32, tag="xo_w")
+        u1_rest = tile("u1_rest", [P, PACK - 1, O], F32, tag="w0_d")
+        u1 = [u1_first[:]] + [u1_rest[:, t, :] for t in range(PACK - 1)]
+        nc.vector.tensor_tensor(u1[0], level[:, 0, :], gate[:, 0, :], ALU.mult)
         a_sb = [tile("a_sb%d" % t, [P, J], F32) for t in range(PACK)]
         for t in range(PACK):
             nc.vector.tensor_copy(a_sb[t][:], a_ps[t][:])
         for t in range(1, PACK):
-            nc.vector.tensor_tensor(u1[:, t, :], level[t][:], gate[t][:], ALU.mult)
+            nc.vector.tensor_tensor(u1[t], level[:, t, :], gate[:, t, :], ALU.mult)
 
         p_sb = [tile("p_sb%d" % h, [P, O], F32) for h in range(2)]
         for half in range(2):
@@ -180,12 +185,13 @@ def tile_list_gatedlevels_bank_one_gatedout_kernel(
                     a_pick[:, t, :], a_sb[t][:].indirect(l5[:, 8 * half : 8 * half + 8]), ACT.Copy,
                     scale=sa_t[:, t : t + 1],
                 )
+            hid_rows = tile("hid_rows%d" % half, [P, PACK, HALF], BF16)
+            for t in range(PACK):
+                nc.vector.tensor_tensor(hid_rows[:, t, :], u1[t][:, cols], a_pick[:, t, :], ALU.max)
             hid = tile("hid%d" % half, [P, HALF * PACK], BF16)
-            nc.vector.tensor_tensor(
+            nc.vector.tensor_copy(
                 hid[:].rearrange("p (c i t) -> p c t i", i=4, t=PACK),
-                u1[:, :, cols].rearrange("p t (c i) -> p c t i", i=4),
-                a_pick[:].rearrange("p t (c i) -> p c t i", i=4),
-                ALU.max,
+                hid_rows[:].rearrange("p t (c i) -> p c t i", i=4),
             )
             codes = tile("codes%d" % half, [P, HALF], U32)
             scales = tile("scales%d" % half, [P, HALF], U8)

@@ -81,17 +81,17 @@ def tile_list_gatedlevels_bank_one_gatedout_kernel(
         nc.sync.dma_start(xo_stage[:], by_quadrant(xo_scales))
         bg_t = load_r_vector("bg_t", bg, nc.gpsimd)
         st_t = load_r_vector("st_t", st, nc.gpsimd)
+        tb_t = [load_tb(0)]
         l4 = load_list("l4", offs4)
         sg_t = load_r_vector("sg_t", sg, nc.sync)
-        tb_t = [load_tb(0)]
         nc.sync.dma_start(w_stage[64:68, :, 0, :], by_quadrant(w_scales))
         nc.sync.dma_start(w_stage[64:68, :, 1, :], by_quadrant(w0_scales))
         tb_t.append(load_tb(1))
         w_w = load_words("w_w", w_words[0], U8, 2 * R)
         w0_w = load_words("w0_w", w0_words[0], U8, 2 * R)
         l1 = load_list("l1", offs)
-        l2 = load_list("l2", offs2)
         xt_w = load_words("xt_w", xt_words[0].rearrange("p n t -> p (n t)"), U32, T)
+        l2 = load_list("l2", offs2)
         l3 = load_list("l3", offs3)
         xo_w = load_words("xo_w", xo_words[0].rearrange("p n t -> p (n t)"), U32, T)
         tb_t.append(load_tb(2))

from contextlib import ExitStack

import concourse.mybir as mybir

F32 = mybir.dt.float32
BF16 = mybir.dt.bfloat16
I32 = mybir.dt.int32
U32 = mybir.dt.uint32
U16 = mybir.dt.uint16
U8 = mybir.dt.uint8
E4M3X4 = mybir.dt.float8_e4m3fn_x4
E5M2X4 = mybir.dt.float8_e5m2_x4
E2M1X4 = mybir.dt.float4_e2m1fn_x4
ACT = mybir.ActivationFunctionType
ALU = mybir.AluOpType

P = 128
PACK = 4
QUADS = 4
T, J, R, X, O, N, U = 1024, 256, 512, 1024, 256, 256, 128
HALF = O // 2
FLOPS = 2 * (2 * 512 * R * J + R * N * O)


def tile_list_gatedlevels_bank_one_gatedout_kernel(
    tc, xt_words, xt_scales, xo_words, xo_scales, w_words, w_scales, w0_words, w0_scales,
    tb, st, sa, sg, bg, wb_words, wb_scales, so, sp, bo,
    offs, offs2, offs3, offs4, offs5, offs6, offs7, out,
):
    nc = tc.nc
    with ExitStack() as ctx:
        sb = ctx.enter_context(tc.tile_pool(name="sb", bufs=1))
        ps = ctx.enter_context(tc.psum_pool(name="ps", bufs=1))

        def tile(name, shape, dtype, tag=None):
            return sb.tile(shape, dtype, name=name, tag=tag or name, align_bytes=64)

        def load_list(name, src):
            t = sb.tile(list(src.shape), U16, name=name)
            nc.sync.dma_start(t[:], src)
            return t

        def load_words(name, src, dtype, columns):
            t = tile(name, [P, columns], dtype)
            nc.sync.dma_start(t[:].bitcast(I32), src.bitcast(I32))
            return t

        def by_quadrant(scales):
            return scales[0].bitcast(I32).rearrange("(q r) n -> r q n", r=4)

        def load_r_vector(name, src, queue):
            t = tile(name, [P, PACK], F32)
            queue.dma_start(t[:], src.rearrange("(p t) o -> p (t o)", t=PACK))
            return t

        def load_n_vector(name, src):
            t = tile(name, [P, 2], F32)
            with nc.allow_non_contiguous_dma(reason="one value a partition"):
                nc.sync.dma_start(t[:], src.rearrange("(h p) o -> p (h o)", p=P))
            return t

        tb_rows = tb.rearrange("(p t) x -> t p x", t=PACK)

        def load_tb(t):
            rows = tile("tb%d" % t, [P, X], F32)
            nc.sync.dma_start(rows[:], tb_rows[t])
            return rows

        w_stage = tile("w_stage", [P, QUADS, 2, R // 4], I32)
        xt_plane = tile("xt_plane", [P, T], U8)
        xo_plane = tile("xo_plane", [P, T], U8)
        wb_plane = tile("wb_plane", [P, N], U8)
        nc.vector.memset(w_stage[64:96], 0)
        nc.vector.memset(xt_plane[:].bitcast(I32), 0)
        nc.vector.memset(xo_plane[:].bitcast(I32), 0)
        nc.vector.memset(wb_plane[:].bitcast(I32), 0)

        xt_stage = tile("xt_stage", [4, QUADS, T // 4], I32)
        xo_stage = tile("xo_stage", [4, QUADS, T // 4], I32)
        nc.sync.dma_start(xt_stage[:], by_quadrant(xt_scales))
        nc.sync.dma_start(xo_stage[:], by_quadrant(xo_scales))
        bg_t = load_r_vector("bg_t", bg, nc.gpsimd)
        st_t = load_r_vector("st_t", st, nc.gpsimd)
        tb_t = [load_tb(0)]
        l4 = load_list("l4", offs4)
        sg_t = load_r_vector("sg_t", sg, nc.sync)
        nc.sync.dma_start(w_stage[64:68, :, 0, :], by_quadrant(w_scales))
        nc.sync.dma_start(w_stage[64:68, :, 1, :], by_quadrant(w0_scales))
        tb_t.append(load_tb(1))
        w_w = load_words("w_w", w_words[0], U8, 2 * R)
        w0_w = load_words("w0_w", w0_words[0], U8, 2 * R)
        l1 = load_list("l1", offs)
        xt_w = load_words("xt_w", xt_words[0].rearrange("p n t -> p (n t)"), U32, T)
        l2 = load_list("l2", offs2)
        l3 = load_list("l3", offs3)
        xo_w = load_words("xo_w", xo_words[0].rearrange("p n t -> p (n t)"), U32, T)
        tb_t.append(load_tb(2))
        tb_t.append(load_tb(3))
        l5 = load_list("l5", offs5)
        sa_t = load_r_vector("sa_t", sa, nc.sync)
        wb_w = load_words("wb_w", wb_words[0], U8, 2 * N)
        for q in range(QUADS):
            nc.sync.dma_start(
                wb_plane[32 * q : 32 * q + 4, :].bitcast(I32),
                wb_scales[0, 4 * q : 4 * q + 4, :].bitcast(I32),
            )
        l7 = load_list("l7", offs7)
        l6 = load_list("l6", offs6)
        sp_t = load_n_vector("sp_t", sp)
        bo_t = load_n_vector("bo_t", bo)
        so_t = load_n_vector("so_t", so)

        for q in range(QUADS):
            for stage, plane in ((xo_stage, xo_plane), (xt_stage, xt_plane)):
                nc.vector.tensor_copy(plane[32 * q : 32 * q + 4, :].bitcast(I32), stage[:, q, :])
        w_plane = tile("w_plane", [P, 2 * R], U8)
        for q in range(QUADS):
            nc.vector.tensor_copy(
                w_plane[32 * q : 32 * q + 32, :].bitcast(I32),
                w_stage[64:96, q].rearrange("p m n -> p (m n)"),
            )
        w_sc = tile("w_sc", [P, 2, PACK, P], U8)
        nc.vector.tensor_copy(w_sc[:], w_plane[:].rearrange("p (m c t) -> p m t c", m=2, t=PACK))

        gate = tile("gate", [P, PACK, O], F32)
        level = tile("level", [P, PACK, O], F32)

        def look_up_levels(t):
            nc.scalar.activation(
                gate[:, t, :], tb_t[t][:].indirect(l4[:]), ACT.Sigmoid,
                bias=bg_t[:, t : t + 1], scale=sg_t[:, t : t + 1],
            )
            nc.scalar.activation(level[:, t, :], tb_t[t][:].indirect(l3[:]), ACT.Copy, scale=st_t[:, t : t + 1])

        def pick(name, words, plane, lst):
            g_sc = tile(name + "_gs", [P, J], U8)
            g_w = tile(name + "_gw", [P, J], U32)
            nc.vector.tensor_copy(g_sc[:], plane[:].indirect(lst[:]))
            nc.vector.tensor_copy(g_w[:], words[:].indirect(lst[:]))
            return g_w, g_sc

        def deal(name, src):
            dealt = tile(name, [P, 2 * R], U8)
            nc.scalar.copy(
                dealt[:].bitcast(U16).rearrange("p (t c) -> p t c", t=PACK),
                src[:].bitcast(U16).rearrange("p (c t) -> p t c", t=PACK),
            )
            return dealt

        look_up_levels(0)
        look_up_levels(1)
        w_d = [deal("w_d", w_w), deal("w0_d", w0_w)]
        look_up_levels(2)
        look_up_levels(3)
        picked = [pick("xt", xt_w, xt_plane, l1), pick("xo", xo_w, xo_plane, l2)]
        a_ps = [ps.tile([P, J], F32, name="a_ps%d" % t) for t in range(PACK)]
        for m, fmt in enumerate((E5M2X4, E4M3X4)):
            g_w, g_sc = picked[m]
            for t in range(PACK):
                nc.tensor.matmul_mx(
                    a_ps[t][:],
                    lhsT=w_d[m][:, 2 * P * t : 2 * P * (t + 1)].bitcast(E2M1X4),
                    lhsT_scale=w_sc[:, m, t, :],
                    rhs=g_w[:].bitcast(fmt),
                    rhs_scale=g_sc[:],
                    start=(m == 0),
                    stop=(m == 1),
                )
        u1_first = tile("u1_first", [P, O], F32, tag="xo_w")
        u1_rest = tile("u1_rest", [P, PACK - 1, O], F32, tag="w0_d")
        u1 = [u1_first[:]] + [u1_rest[:, t, :] for t in range(PACK - 1)]
        nc.vector.tensor_tensor(u1[0], level[:, 0, :], gate[:, 0, :], ALU.mult)
        a_sb = [tile("a_sb%d" % t, [P, J], F32) for t in range(PACK)]
        for t in range(PACK):
            nc.vector.tensor_copy(a_sb[t][:], a_ps[t][:])
        for t in range(1, PACK):
            nc.vector.tensor_tensor(u1[t], level[:, t, :], gate[:, t, :], ALU.mult)

        p_sb = [tile("p_sb%d" % h, [P, O], F32) for h in range(2)]
        for half in range(2):
            cols = slice(half * HALF, (half + 1) * HALF)
            a_pick = tile("a_pick%d" % half, [P, PACK, HALF], F32)
            for t in range(PACK):
                nc.scalar.activation(
                    a_pick[:, t, :], a_sb[t][:].indirect(l5[:, 8 * half : 8 * half + 8]), ACT.Copy,
                    scale=sa_t[:, t : t + 1],
                )
            hid_rows = tile("hid_rows%d" % half, [P, PACK, HALF], BF16)
            for t in range(PACK):
                nc.vector.tensor_tensor(hid_rows[:, t, :], u1[t][:, cols], a_pick[:, t, :], ALU.max)
            hid = tile("hid%d" % half, [P, HALF * PACK], BF16)
            nc.vector.tensor_copy(
                hid[:].rearrange("p (c i t) -> p c t i", i=4, t=PACK),
                hid_rows[:].rearrange("p t (c i) -> p c t i", i=4),
            )
            codes = tile("codes%d" % half, [P, HALF], U32)
            scales = tile("scales%d" % half, [P, HALF], U8)
            nc.vector.quantize_mx(codes[:].bitcast(E4M3X4), scales[:], hid[:])
            for h in range(2):
                p_ps = ps.tile([P, HALF], F32, name="p_ps%d%d" % (half, h))
                nc.tensor.matmul_mx(
                    p_ps[:],
                    lhsT=wb_w[:, 2 * P * h : 2 * P * (h + 1)].bitcast(E2M1X4),
                    lhsT_scale=wb_plane[:, P * h : P * (h + 1)],
                    rhs=codes[:].bitcast(E4M3X4),
                    rhs_scale=scales[:],
                    start=True,
                    stop=True,
                )
                nc.vector.tensor_copy(p_sb[h][:, cols], p_ps[:])

        for h in range(2):
            g = tile("out_gate%d" % h, [P, U], F32)
            v = tile("out_value%d" % h, [P, U], F32)
            y = tile("y%d" % h, [P, U], F32)
            nc.scalar.activation(
                g[:], p_sb[h][:].indirect(l7[:]), ACT.Sigmoid,
                bias=bo_t[:, h : h + 1], scale=sp_t[:, h : h + 1],
            )
            nc.scalar.activation(v[:], p_sb[h][:].indirect(l6[:]), ACT.Copy, scale=so_t[:, h : h + 1])
            nc.vector.tensor_tensor(y[:], v[:], g[:], ALU.mult)
            nc.sync.dma_start(out[P * h : P * (h + 1), :], y[:])
